import numpy as np
import ml_dtypes


def mxq(x, axis, fmt="e4m3"):
    dtype, down = {"e4m3": (ml_dtypes.float8_e4m3fn, 7), "e5m2": (ml_dtypes.float8_e5m2, 14)}[fmt]
    v = np.moveaxis(np.asarray(x, np.float32).astype(ml_dtypes.bfloat16).astype(np.float64), axis, -1)
    blocks = v.reshape(v.shape[:-1] + (-1, 32))
    amax = np.abs(blocks).max(-1, keepdims=True)
    byte = np.maximum(np.where(amax > 0, np.frexp(amax)[1] - 1 + 127, 0) - down, 1)
    scale = np.exp2(byte - 127.0)
    codes = (blocks / scale).astype(np.float32).astype(dtype).astype(np.float64)
    return np.moveaxis((codes * scale).reshape(v.shape), -1, axis)


WIDE = False


def mx_kscale(k):
    if not WIDE:
        return np.ones(k)
    levels = np.array([10, -10, 5, -5, 0])
    if k % 512:
        return np.exp2(np.random.permutation(np.resize(levels, k // 32))).repeat(32)
    a = np.empty((k // 512, 16))
    for p in range(k // 512):
        a[p, :8] = np.random.permutation(np.resize(levels, 8))
        for g in range(8):
            far = levels[np.abs(levels - a[p, g]) >= 10]
            a[p, g + 8] = far[np.random.randint(len(far))]
    return np.exp2(a.ravel()).repeat(32)


def f64(x):
    return np.asarray(x).astype(np.float64)


def striped(idx):
    return np.tile(idx.reshape(-1, 16).T, (8, 1)).astype(np.uint16)


def unstriped(offs):
    return offs[:16].T.reshape(-1).astype(np.int64)


def pack_weight(w):
    k, n = w.shape
    w = f64(np.asarray(w, np.float32).astype(ml_dtypes.bfloat16)).reshape(k // 32, 32, n)
    amax = np.abs(w).max(1)
    byte = np.clip(np.where(amax > 0, np.frexp(amax)[1] - 1 + 127 - 7, 1), 1, 254)
    scaled = (w * np.exp2(127.0 - byte)[:, None, :]).reshape(k, n).astype(np.float32)
    words = np.ascontiguousarray(scaled.reshape(k // 512, 128, 4, n).transpose(0, 1, 3, 2)).astype(ml_dtypes.float8_e4m3fn).view(np.uint8)
    return words, np.ascontiguousarray(byte.astype(np.uint8).reshape(k // 512, 16, n))


def unpack_weight(words, scales):
    g, p, n, _ = words.shape
    vals = np.ascontiguousarray(words).view(ml_dtypes.float8_e4m3fn).astype(np.float64) * np.repeat(np.exp2(scales.astype(np.float64) - 127.0), 8, axis=1)[..., None]
    return vals.transpose(0, 1, 3, 2).reshape(g * 512, n)


E2M1 = np.array([0.0, 0.5, 1.0, 1.5, 2.0, 3.0, 4.0, 6.0, -0.0, -0.5, -1.0, -1.5, -2.0, -3.0, -4.0, -6.0])


def pack_fp4(w):
    k, n = w.shape
    w = f64(np.asarray(w, np.float32).astype(ml_dtypes.bfloat16)).reshape(k // 32, 32, n)
    amax = np.abs(w).max(1)
    mant, ex = np.frexp(amax / 6.0)
    byte = np.clip(np.where(amax > 0, np.where(mant > 0.5, ex, ex - 1) + 127, 1), 1, 254)
    scaled = (w * np.exp2(127.0 - byte)[:, None, :]).reshape(k, n).astype(np.float32)
    c = np.ascontiguousarray(scaled.reshape(k // 512, 128, 4, n).transpose(0, 1, 3, 2)).astype(ml_dtypes.float4_e2m1fn).view(np.uint8) & 0xF
    words = (c[..., 0::2] | (c[..., 1::2] << 4)).reshape(k // 512, 128, 2 * n)
    return np.ascontiguousarray(words), np.ascontiguousarray(byte.astype(np.uint8).reshape(k // 512, 16, n))


def unpack_fp4(words, scales):
    g, _, n = scales.shape
    words = np.ascontiguousarray(words).reshape(g, 128, n, 2)
    nib = np.empty((g, 128, n, 4), np.uint8)
    nib[..., 0::2] = words & 0xF
    nib[..., 1::2] = words >> 4
    vals = E2M1[nib] * np.repeat(np.exp2(scales.astype(np.float64) - 127.0), 8, axis=1)[..., None]
    return vals.transpose(0, 1, 3, 2).reshape(g * 512, n)


def relu(v):
    return np.maximum(v, 0.0)


K, T, S, D, N, H = 1024, 2048, 512, 4, 256, 512


def setup_inputs():
    n = np.random.standard_normal
    s = mx_kscale(K)[:, None]
    u = mx_kscale(H)
    packed_xT = pack_weight(n((K, T)) * s)
    packed_w1 = pack_fp4(n((K, H)) / np.sqrt(K) / s)
    packed_w2 = pack_fp4(n((K, H)) / np.sqrt(K) / s)
    packed_w3 = pack_fp4(n((H, N)) / np.sqrt(H) / u[:, None])
    return {
        "x_words": packed_xT[0],
        "x_scales": packed_xT[1],
        "w1_words": packed_w1[0],
        "w1_scales": packed_w1[1],
        "w2_words": packed_w2[0],
        "w2_scales": packed_w2[1],
        "lodf": (np.random.uniform(-0.6, 0.6, (H, S))).astype(np.float32),
        "unit": (np.random.uniform(0.6, 1.4, (H, 1)) * u[:, None]).astype(np.float32),
        "w3_words": packed_w3[0],
        "w3_scales": packed_w3[1],
        "offs": striped(np.random.permutation(T)[:S]),
        "out_l": striped(np.random.permutation(S)),
    }


def reference(x_words, x_scales, w1_words, w1_scales, w2_words, w2_scales, lodf, unit, w3_words, w3_scales, offs, out_l):
    xq = unpack_weight(x_words, x_scales)[:, unstriped(offs)]
    fl = unpack_fp4(w1_words, w1_scales).T @ xq
    fo = fl[:, unstriped(out_l)]
    post = fl + fo * f64(lodf)
    lm = unpack_fp4(w2_words, w2_scales).T @ xq
    cap = np.log(np.exp(lm) + 1.0) + 0.5
    over = relu(np.abs(post) - cap)
    tot = over.reshape(len(over), -1, D).sum(axis=2)
    shr = over / (np.repeat(tot, D, axis=1) + 0.3)
    hid = f64(unit) * (shr * post + 0.5 * np.tanh(post))
    return unpack_fp4(w3_words, w3_scales).T @ mxq(hid, 0, "e4m3")

@@ -1,0 +1,192 @@
+from contextlib import ExitStack
+
+import concourse.mybir as mybir
+
+K, T, S, D, N, H = 1024, 2048, 512, 4, 256, 512
+FLOPS = 2 * (2 * K * H * S + H * N * S)
+
+F32 = mybir.dt.float32
+BF16 = mybir.dt.bfloat16
+I32 = mybir.dt.int32
+U32 = mybir.dt.uint32
+U16 = mybir.dt.uint16
+U8 = mybir.dt.uint8
+FP8X4 = mybir.dt.float8_e4m3fn_x4
+FP4X4 = mybir.dt.float4_e2m1fn_x4
+ALU = mybir.AluOpType
+ACT = mybir.ActivationFunctionType
+
+P = 128
+PACK = 4
+PASSES = K // (P * PACK)
+V = S // D
+HALF = S // 2
+CLAMP = 40.0
+
+
+def tile_picked_ylopfw_shr_p_kernel(tc, x_words, x_scales, w1_words, w1_scales, w2_words, w2_scales,
+        lodf, unit, w3_words, w3_scales, offs, out_l, out):
+    nc = tc.nc
+    with ExitStack() as ctx:
+        keep = ctx.enter_context(tc.tile_pool(name="keep", bufs=1))
+        psum = ctx.enter_context(tc.psum_pool(name="psum", bufs=1))
+
+        def sb(name, shape, dtype, tag=None):
+            return keep.tile(shape, dtype, name=name, tag=tag or name, align_bytes=64)
+
+        def load_scale_rows(queue, tile, scales):
+            for q in range(4):
+                queue.dma_start(out=tile[32 * q : 32 * q + 4].bitcast(I32),
+                                in_=scales[:, 4 * q : 4 * q + 4, :].rearrange("o r c -> r o c").bitcast(I32))
+
+        offs_sb = sb("offs_sb", [P, S // 16], U16)
+        outl_sb = sb("outl_sb", [P, S // 16], U16)
+        xs = sb("xs", [P, T], U8)
+        raw_w = [sb(f"raw_w{i}", [P, PASSES, 2 * H], U8, tag=f"stage{i}") for i in range(2)]
+        raw_s = sb("raw_s", [P, PASSES, H], U8)
+        gs = [sb(f"gs{g}", [P, S], U8) for g in range(PASSES)]
+        dw = [sb(f"dw{i}", [P, PASSES, 2 * H], U8) for i in range(2)]
+        ds = [sb(f"ds{i}", [P, PASSES, H], U8) for i in range(2)]
+
+        def load_x(g, tag):
+            tile = sb(f"xw{g}", [P, T], I32, tag=tag)
+            nc.sync.dma_start(out=tile[:], in_=x_words[g].rearrange("p n t -> p (n t)").bitcast(I32))
+            return tile
+
+        def deal_words(i):
+            dst = dw[i][:].bitcast(U16).rearrange("p o (t m) -> p o t m", t=PACK)
+            src = raw_w[i][:].bitcast(U16).rearrange("p o (m t) -> p o t m", t=PACK)
+            nc.scalar.copy(dst, src)
+
+        def deal_scales(i):
+            nc.vector.tensor_copy(out=ds[i][:].rearrange("p o (t m) -> p o t m", t=PACK),
+                                  in_=raw_s[:].rearrange("p o (m t) -> p o t m", t=PACK))
+
+        fl = [sb(f"fl{t}", [P, S + 16], F32) for t in range(PACK)]
+        nc.vector.memset(xs[:].bitcast(I32), 0)
+        nc.vector.memset(raw_s[:].bitcast(I32), 0)
+        nc.gpsimd.memset(gs[1][:].bitcast(I32), 0)
+        for t in range(PACK):
+            nc.gpsimd.memset(fl[t][:, S:], 0.0)
+
+        nc.sync.dma_start(offs_sb[:], offs)
+        nc.sync.dma_start(out=raw_w[0][:].bitcast(I32), in_=w1_words.rearrange("o p c -> p o c").bitcast(I32))
+        nc.sync.dma_start(outl_sb[:], out_l)
+        for q in range(4):
+            nc.sync.dma_start(out=xs[32 * q : 32 * q + 8, :].bitcast(I32), in_=x_scales[:, 4 * q : 4 * q + 4, :].bitcast(I32))
+        xw0 = load_x(0, "xw0")
+        load_scale_rows(nc.sync, raw_s, w1_scales)
+        xw1 = load_x(1, "xw1")
+        nc.sync.dma_start(out=raw_w[1][:].bitcast(I32), in_=w2_words.rearrange("o p c -> p o c").bitcast(I32))
+
+        deal_words(0)
+        nc.vector.tensor_copy(gs[0][:], xs[:].indirect(offs_sb[:]))
+        for q in range(4):
+            nc.scalar.dma_start(out=gs[1][32 * q : 32 * q + 4, :].bitcast(I32), in_=gs[0][32 * q + 4 : 32 * q + 8, :].bitcast(I32))
+        lodf_v = lodf.rearrange("(p t) j -> p t j", t=PACK)
+        lo = [sb("lo0", [P, 2, S], F32, tag="xs")]
+        nc.sync.dma_start(out=lo[0][:], in_=lodf_v[:, 0:2, :])
+        deal_scales(0)
+        load_scale_rows(nc.sync, raw_s, w2_scales)
+        gw = [sb(f"gw{g}", [P, S], U32) for g in range(PASSES)]
+        nc.vector.tensor_copy(gw[0][:], xw0[:].bitcast(U32).indirect(offs_sb[:]))
+        nc.vector.tensor_copy(gw[1][:], xw1[:].bitcast(U32).indirect(offs_sb[:]))
+        deal_words(1)
+        deal_scales(1)
+        lo.append(sb("lo1", [P, 2, S], F32, tag="xw0"))
+        nc.sync.dma_start(out=lo[1][:], in_=lodf_v[:, 2:4, :])
+        u = sb("u", [P, PACK], F32, tag="xw1")
+        nc.sync.dma_start(out=u[:], in_=unit.rearrange("(p t) o -> p (t o)", t=PACK))
+        w3w = sb("w3w", [P, 2 * N], U8, tag="stage1")
+        nc.sync.dma_start(out=w3w[:].bitcast(I32), in_=w3_words[0].bitcast(I32))
+        w3s = raw_s[:, 0:1, 0:N]
+        load_scale_rows(nc.sync, w3s, w3_scales)
+
+        uh = sb("uh", [P, PACK], F32)
+        nc.scalar.mul(uh[:], u[:], 0.5)
+
+        banks = [[psum.tile([P, S], F32, name=f"bank{i}{t}", tag=f"bank{i}{t}") for t in range(PACK)] for i in range(2)]
+        for i in range(2):
+            for t in [(k + i) % PACK for k in range(PACK)]:
+                for g in range(PASSES):
+                    nc.tensor.matmul_mx(out=banks[i][t][:],
+                                        lhsT=dw[i][:, g, 2 * P * t : 2 * P * (t + 1)].bitcast(FP4X4),
+                                        lhsT_scale=ds[i][:, g, P * t : P * (t + 1)],
+                                        rhs=gw[g][:].bitcast(FP8X4), rhs_scale=gs[g][:],
+                                        start=(g == 0), stop=(g == PASSES - 1))
+        fl_ps, lm_ps = banks
+
+        def by_member(ap):
+            return ap.rearrange("p (v d) -> p d v", d=D)
+
+        def rows(ap):
+            return ap.rearrange("p (d v) -> p d v", d=D)
+
+        def tiles(name):
+            return [sb(f"{name}{t}", [P, S], F32) for t in range(PACK)]
+
+        prod, post, ex, cap, mag, gap, exc, sh = [tiles(n) for n in
+            ("prod", "post", "ex", "cap", "mag", "gap", "exc", "sh")]
+        for t in range(PACK):
+            nc.scalar.copy(fl[t][:, :S], fl_ps[t][:])
+        for t in (1, 2, 3, 0):
+            nc.scalar.activation(rows(ex[t][:]), by_member(lm_ps[t][:]), ACT.Exp)
+        for t in range(PACK):
+            nc.vector.tensor_tensor(prod[t][:], fl[t][:].indirect(outl_sb[:]), lo[t // 2][:, t % 2, :], ALU.mult)
+            nc.vector.tensor_tensor(post[t][:].rearrange("p (d v) -> p v d", d=D),
+                                    prod[t][:].rearrange("p (v d) -> p v d", d=D),
+                                    fl_ps[t][:].rearrange("p (v d) -> p v d", d=D), ALU.add)
+        ln = []
+        for t in range(PACK):
+            ln.append(sb(f"ln{t}", [P, S], F32, tag=f"ex{t - 1}" if t else "ln0"))
+            nc.scalar.activation(ln[t][:], ex[t][:], ACT.Ln, bias=1.0)
+            nc.scalar.activation(mag[t][:], post[t][:], ACT.Abs)
+
+        th = sb("th", [P, PACK, S], F32)
+        rcp = sb("rcp", [P, PACK, V], F32)
+        for t in range(PACK):
+            nc.vector.scalar_tensor_tensor(rows(cap[t][:]), rows(ln[t][:]), CLAMP, by_member(lm_ps[t][:]), ALU.min, ALU.max)
+            nc.vector.scalar_tensor_tensor(gap[t][:], mag[t][:], 0.5, cap[t][:], ALU.subtract, ALU.subtract)
+            upper = sb(f"upper{t}", [P, HALF], F32)
+            pairs = sb(f"pairs{t}", [P, HALF], F32)
+            tot = sb(f"tot{t}", [P, V], F32)
+            nc.vector.tensor_scalar(upper[:], gap[t][:, HALF:], 0.0, None, ALU.max)
+            nc.vector.scalar_tensor_tensor(pairs[:], gap[t][:, :HALF], 0.0, upper[:], ALU.max, ALU.add)
+            nc.vector.scalar_tensor_tensor(tot[:], pairs[:, :V], 0.3, pairs[:, V:], ALU.add, ALU.add)
+            nc.scalar.activation(th[:, t, 0:V], tot[:], ACT.Ln)
+        for t in range(PACK):
+            nc.vector.scalar_tensor_tensor(exc[t][:], gap[t][:], 0.0, post[t][:], ALU.max, ALU.mult)
+        nc.scalar.activation(rcp[:], th[:, :, 0:V], ACT.Exp, scale=-1.0)
+        for t in range(PACK):
+            nc.scalar.activation(th[:, t, :], post[t][:], ACT.Tanh)
+        for t in range(PACK):
+            nc.vector.scalar_tensor_tensor(rows(sh[t][:]), rows(exc[t][:]), u[:, t : t + 1],
+                                           rcp[:, t : t + 1, :].to_broadcast([P, D, V]), ALU.mult, ALU.mult)
+
+        out_ps = [psum.tile([P, S], F32, name=f"outb{m}", tag=f"bank0{m}") for m in range(N // P)]
+        for c in range(2):
+            cols = slice(c * HALF, (c + 1) * HALF)
+            hb = sb(f"hb{c}", [P, PACK, HALF], BF16)
+            for t in range(PACK):
+                nc.vector.scalar_tensor_tensor(hb[:, t, :], th[:, t, cols], uh[:, t : t + 1], sh[t][:, cols], ALU.mult, ALU.add)
+            hi = sb(f"hi{c}", [P, HALF, PACK], BF16)
+            if c == 0:
+                nc.scalar.copy(hi[:], hb[:].rearrange("p t j -> p j t"))
+            else:
+                nc.vector.tensor_copy(hi[:], hb[:].rearrange("p t j -> p j t"))
+            hq = sb(f"hq{c}", [P, HALF], U32)
+            hs = sb(f"hs{c}", [P, HALF], U8)
+            nc.vector.quantize_mx(out=hq[:].bitcast(FP8X4), scales=hs[:], in_=hi[:].rearrange("p j t -> p (j t)"))
+            for m in range(N // P):
+                nc.tensor.matmul_mx(out=out_ps[m][:, cols], lhsT=w3w[:, 2 * P * m : 2 * P * (m + 1)].bitcast(FP4X4),
+                                    lhsT_scale=w3s[:, 0, P * m : P * (m + 1)],
+                                    rhs=hq[:].bitcast(FP8X4), rhs_scale=hs[:], start=True, stop=True)
+        for m in range(N // P):
+            res = sb(f"res{m}", [P, S], F32)
+            src = out_ps[m][:].rearrange("p (d v) -> p v d", d=D)
+            dst = res[:].rearrange("p (v d) -> p v d", d=D)
+            if m == 0:
+                nc.scalar.copy(dst, src)
+            else:
+                nc.vector.tensor_copy(dst, src)
+            (nc.scalar if m == 0 else nc.sync).dma_start(out=out[m * P : (m + 1) * P, :], in_=res[:])

@@ -42,11 +42,11 @@ def tile_picked_ylopfw_shr_p_kernel(tc, x_words, x_scales, w1_words, w1_scales, 
         offs_sb = sb("offs_sb", [P, S // 16], U16)
         outl_sb = sb("outl_sb", [P, S // 16], U16)
         xs = sb("xs", [P, T], U8)
-        raw_w = [sb(f"raw_w{i}", [P, PASSES, 2 * H], U8, tag=f"stage{i}") for i in range(2)]
-        raw_s = sb("raw_s", [P, PASSES, H], U8)
+        raw_w = [sb(f"raw_w{i}", [P, PASSES, 2 * H], U8) for i in range(2)]
+        raw_s = [sb(f"raw_s{i}", [P, PASSES, H], U8) for i in range(2)]
         gs = [sb(f"gs{g}", [P, S], U8) for g in range(PASSES)]
         dw = [sb(f"dw{i}", [P, PASSES, 2 * H], U8) for i in range(2)]
-        ds = [sb(f"ds{i}", [P, PASSES, H], U8) for i in range(2)]
+        ds = [sb("ds0", [P, PASSES, H], U8)]
 
         def load_x(g, tag):
             tile = sb(f"xw{g}", [P, T], I32, tag=tag)
@@ -60,54 +60,53 @@ def tile_picked_ylopfw_shr_p_kernel(tc, x_words, x_scales, w1_words, w1_scales, 
 
         def deal_scales(i):
             nc.vector.tensor_copy(out=ds[i][:].rearrange("p o (t m) -> p o t m", t=PACK),
-                                  in_=raw_s[:].rearrange("p o (m t) -> p o t m", t=PACK))
+                                  in_=raw_s[i][:].rearrange("p o (m t) -> p o t m", t=PACK))
 
         fl = [sb(f"fl{t}", [P, S + 16], F32) for t in range(PACK)]
+        w3s = sb("w3s", [P, 1, N], U8)
         nc.vector.memset(xs[:].bitcast(I32), 0)
-        nc.vector.memset(raw_s[:].bitcast(I32), 0)
+        nc.vector.memset(raw_s[0][:].bitcast(I32), 0)
+        nc.gpsimd.memset(raw_s[1][:].bitcast(I32), 0)
         nc.gpsimd.memset(gs[1][:].bitcast(I32), 0)
+        nc.gpsimd.memset(w3s[:].bitcast(I32), 0)
         for t in range(PACK):
             nc.gpsimd.memset(fl[t][:, S:], 0.0)
 
         nc.sync.dma_start(offs_sb[:], offs)
-        nc.sync.dma_start(out=raw_w[0][:].bitcast(I32), in_=w1_words.rearrange("o p c -> p o c").bitcast(I32))
         nc.sync.dma_start(outl_sb[:], out_l)
+        nc.sync.dma_start(out=raw_w[0][:].bitcast(I32), in_=w1_words.rearrange("o p c -> p o c").bitcast(I32))
         for q in range(4):
             nc.sync.dma_start(out=xs[32 * q : 32 * q + 8, :].bitcast(I32), in_=x_scales[:, 4 * q : 4 * q + 4, :].bitcast(I32))
         xw0 = load_x(0, "xw0")
-        load_scale_rows(nc.sync, raw_s, w1_scales)
+        load_scale_rows(nc.sync, raw_s[0], w1_scales)
         xw1 = load_x(1, "xw1")
         nc.sync.dma_start(out=raw_w[1][:].bitcast(I32), in_=w2_words.rearrange("o p c -> p o c").bitcast(I32))
+        load_scale_rows(nc.gpsimd, raw_s[1], w2_scales)
+        load_scale_rows(nc.gpsimd, w3s, w3_scales)
 
         deal_words(0)
         nc.vector.tensor_copy(gs[0][:], xs[:].indirect(offs_sb[:]))
         for q in range(4):
-            nc.scalar.dma_start(out=gs[1][32 * q : 32 * q + 4, :].bitcast(I32), in_=gs[0][32 * q + 4 : 32 * q + 8, :].bitcast(I32))
+            nc.sync.dma_start(out=gs[1][32 * q : 32 * q + 4, :].bitcast(I32), in_=gs[0][32 * q + 4 : 32 * q + 8, :].bitcast(I32))
         lodf_v = lodf.rearrange("(p t) j -> p t j", t=PACK)
         lo = [sb("lo0", [P, 2, S], F32, tag="xs")]
         nc.sync.dma_start(out=lo[0][:], in_=lodf_v[:, 0:2, :])
         deal_scales(0)
-        load_scale_rows(nc.sync, raw_s, w2_scales)
         gw = [sb(f"gw{g}", [P, S], U32) for g in range(PASSES)]
         nc.vector.tensor_copy(gw[0][:], xw0[:].bitcast(U32).indirect(offs_sb[:]))
-        nc.vector.tensor_copy(gw[1][:], xw1[:].bitcast(U32).indirect(offs_sb[:]))
-        deal_words(1)
-        deal_scales(1)
         lo.append(sb("lo1", [P, 2, S], F32, tag="xw0"))
         nc.sync.dma_start(out=lo[1][:], in_=lodf_v[:, 2:4, :])
-        u = sb("u", [P, PACK], F32, tag="xw1")
-        nc.sync.dma_start(out=u[:], in_=unit.rearrange("(p t) o -> p (t o)", t=PACK))
-        w3w = sb("w3w", [P, 2 * N], U8, tag="stage1")
-        nc.sync.dma_start(out=w3w[:].bitcast(I32), in_=w3_words[0].bitcast(I32))
-        w3s = raw_s[:, 0:1, 0:N]
-        load_scale_rows(nc.sync, w3s, w3_scales)
-
-        uh = sb("uh", [P, PACK], F32)
-        nc.scalar.mul(uh[:], u[:], 0.5)
+        nc.vector.tensor_copy(gw[1][:], xw1[:].bitcast(U32).indirect(offs_sb[:]))
+        deal_words(1)
+        ds.append(sb("ds1", [P, PASSES, H], U8, tag="xw1"))
+        deal_scales(1)
+        w3w = raw_w[1][:, 0, 0 : 2 * N]
+        nc.sync.dma_start(out=w3w.bitcast(I32), in_=w3_words[0].bitcast(I32))
 
         banks = [[psum.tile([P, S], F32, name=f"bank{i}{t}", tag=f"bank{i}{t}") for t in range(PACK)] for i in range(2)]
-        for i in range(2):
-            for t in [(k + i) % PACK for k in range(PACK)]:
+        order = [(0, 0), (0, 1), (1, 1), (1, 2), (0, 2), (1, 3), (1, 0), (0, 3)]
+        for i, t in order:
+            if True:
                 for g in range(PASSES):
                     nc.tensor.matmul_mx(out=banks[i][t][:],
                                         lhsT=dw[i][:, g, 2 * P * t : 2 * P * (t + 1)].bitcast(FP4X4),
@@ -115,6 +114,10 @@ def tile_picked_ylopfw_shr_p_kernel(tc, x_words, x_scales, w1_words, w1_scales, 
                                         rhs=gw[g][:].bitcast(FP8X4), rhs_scale=gs[g][:],
                                         start=(g == 0), stop=(g == PASSES - 1))
         fl_ps, lm_ps = banks
+        u = sb("u", [P, PACK], F32, tag="gs0")
+        nc.sync.dma_start(out=u[:], in_=unit.rearrange("(p t) o -> p (t o)", t=PACK))
+        uh = sb("uh", [P, PACK], F32)
+        nc.scalar.mul(uh[:], u[:], 0.5)
 
         def by_member(ap):
             return ap.rearrange("p (v d) -> p d v", d=D)
@@ -127,25 +130,28 @@ def tile_picked_ylopfw_shr_p_kernel(tc, x_words, x_scales, w1_words, w1_scales, 
 
         prod, post, ex, cap, mag, gap, exc, sh = [tiles(n) for n in
             ("prod", "post", "ex", "cap", "mag", "gap", "exc", "sh")]
-        for t in range(PACK):
-            nc.scalar.copy(fl[t][:, :S], fl_ps[t][:])
-        for t in (1, 2, 3, 0):
-            nc.scalar.activation(rows(ex[t][:]), by_member(lm_ps[t][:]), ACT.Exp)
-        for t in range(PACK):
-            nc.vector.tensor_tensor(prod[t][:], fl[t][:].indirect(outl_sb[:]), lo[t // 2][:, t % 2, :], ALU.mult)
+        def add_flow(t):
             nc.vector.tensor_tensor(post[t][:].rearrange("p (d v) -> p v d", d=D),
                                     prod[t][:].rearrange("p (v d) -> p v d", d=D),
                                     fl_ps[t][:].rearrange("p (v d) -> p v d", d=D), ALU.add)
-        ln = []
-        for t in range(PACK):
-            ln.append(sb(f"ln{t}", [P, S], F32, tag=f"ex{t - 1}" if t else "ln0"))
-            nc.scalar.activation(ln[t][:], ex[t][:], ACT.Ln, bias=1.0)
-            nc.scalar.activation(mag[t][:], post[t][:], ACT.Abs)
+
+        last = PACK - 1
+        for i, t in order[:-1]:
+            if i == 0:
+                nc.scalar.copy(fl[t][:, :S], fl_ps[t][:])
+            else:
+                nc.scalar.activation(rows(ex[t][:]), by_member(lm_ps[t][:]), ACT.Exp)
+        for t in range(last):
+            nc.vector.tensor_tensor(prod[t][:], fl[t][:].indirect(outl_sb[:]), lo[t // 2][:, t % 2, :], ALU.mult)
+            add_flow(t)
 
         th = sb("th", [P, PACK, S], F32)
         rcp = sb("rcp", [P, PACK, V], F32)
         for t in range(PACK):
-            nc.vector.scalar_tensor_tensor(rows(cap[t][:]), rows(ln[t][:]), CLAMP, by_member(lm_ps[t][:]), ALU.min, ALU.max)
+            ln = sb(f"ln{t}", [P, S], F32, tag=f"ex{t - 1}" if t else "ln0")
+            nc.scalar.activation(ln[:], ex[t][:], ACT.Ln, bias=1.0)
+            nc.scalar.activation(mag[t][:], post[t][:], ACT.Abs)
+            nc.vector.scalar_tensor_tensor(rows(cap[t][:]), rows(ln[:]), CLAMP, by_member(lm_ps[t][:]), ALU.min, ALU.max)
             nc.vector.scalar_tensor_tensor(gap[t][:], mag[t][:], 0.5, cap[t][:], ALU.subtract, ALU.subtract)
             upper = sb(f"upper{t}", [P, HALF], F32)
             pairs = sb(f"pairs{t}", [P, HALF], F32)
@@ -154,6 +160,12 @@ def tile_picked_ylopfw_shr_p_kernel(tc, x_words, x_scales, w1_words, w1_scales, 
             nc.vector.scalar_tensor_tensor(pairs[:], gap[t][:, :HALF], 0.0, upper[:], ALU.max, ALU.add)
             nc.vector.scalar_tensor_tensor(tot[:], pairs[:, :V], 0.3, pairs[:, V:], ALU.add, ALU.add)
             nc.scalar.activation(th[:, t, 0:V], tot[:], ACT.Ln)
+            if t == 0:
+                nc.scalar.copy(fl[last][:, :S], fl_ps[last][:])
+                fo = sb("fo", [P, S], F32, tag="ln0")
+                nc.scalar.activation(fo[:], fl[last][:].indirect(outl_sb[:]), ACT.Copy)
+                nc.vector.tensor_tensor(prod[last][:], fo[:], lo[last // 2][:, last % 2, :], ALU.mult)
+                add_flow(last)
         for t in range(PACK):
             nc.vector.scalar_tensor_tensor(exc[t][:], gap[t][:], 0.0, post[t][:], ALU.max, ALU.mult)
         nc.scalar.activation(rcp[:], th[:, :, 0:V], ACT.Exp, scale=-1.0)

@@ -63,14 +63,13 @@ def tile_picked_ylopfw_shr_p_kernel(tc, x_words, x_scales, w1_words, w1_scales, 
                                   in_=raw_s[i][:].rearrange("p o (m t) -> p o t m", t=PACK))
 
         fl = [sb(f"fl{t}", [P, S + 16], F32) for t in range(PACK)]
-        w3s = sb("w3s", [P, 1, N], U8)
         nc.vector.memset(xs[:].bitcast(I32), 0)
         nc.vector.memset(raw_s[0][:].bitcast(I32), 0)
+        nc.vector.memset(gs[1][:].bitcast(I32), 0)
         nc.gpsimd.memset(raw_s[1][:].bitcast(I32), 0)
-        nc.gpsimd.memset(gs[1][:].bitcast(I32), 0)
-        nc.gpsimd.memset(w3s[:].bitcast(I32), 0)
+        load_scale_rows(nc.gpsimd, raw_s[1], w2_scales)
         for t in range(PACK):
-            nc.gpsimd.memset(fl[t][:, S:], 0.0)
+            nc.vector.memset(fl[t][:, S:], 0.0)
 
         nc.sync.dma_start(offs_sb[:], offs)
         nc.sync.dma_start(outl_sb[:], out_l)
@@ -81,8 +80,6 @@ def tile_picked_ylopfw_shr_p_kernel(tc, x_words, x_scales, w1_words, w1_scales, 
         load_scale_rows(nc.sync, raw_s[0], w1_scales)
         xw1 = load_x(1, "xw1")
         nc.sync.dma_start(out=raw_w[1][:].bitcast(I32), in_=w2_words.rearrange("o p c -> p o c").bitcast(I32))
-        load_scale_rows(nc.gpsimd, raw_s[1], w2_scales)
-        load_scale_rows(nc.gpsimd, w3s, w3_scales)
 
         deal_words(0)
         nc.vector.tensor_copy(gs[0][:], xs[:].indirect(offs_sb[:]))
@@ -91,17 +88,19 @@ def tile_picked_ylopfw_shr_p_kernel(tc, x_words, x_scales, w1_words, w1_scales, 
         lodf_v = lodf.rearrange("(p t) j -> p t j", t=PACK)
         lo = [sb("lo0", [P, 2, S], F32, tag="xs")]
         nc.sync.dma_start(out=lo[0][:], in_=lodf_v[:, 0:2, :])
-        deal_scales(0)
         gw = [sb(f"gw{g}", [P, S], U32) for g in range(PASSES)]
         nc.vector.tensor_copy(gw[0][:], xw0[:].bitcast(U32).indirect(offs_sb[:]))
         lo.append(sb("lo1", [P, 2, S], F32, tag="xw0"))
         nc.sync.dma_start(out=lo[1][:], in_=lodf_v[:, 2:4, :])
+        deal_scales(0)
         nc.vector.tensor_copy(gw[1][:], xw1[:].bitcast(U32).indirect(offs_sb[:]))
         deal_words(1)
         ds.append(sb("ds1", [P, PASSES, H], U8, tag="xw1"))
         deal_scales(1)
         w3w = raw_w[1][:, 0, 0 : 2 * N]
         nc.sync.dma_start(out=w3w.bitcast(I32), in_=w3_words[0].bitcast(I32))
+        w3s = raw_s[1][:, 0:1, 0:N]
+        load_scale_rows(nc.sync, w3s, w3_scales)
 
         banks = [[psum.tile([P, S], F32, name=f"bank{i}{t}", tag=f"bank{i}{t}") for t in range(PACK)] for i in range(2)]
         order = [(0, 0), (0, 1), (1, 1), (1, 2), (0, 2), (1, 3), (1, 0), (0, 3)]
@@ -119,86 +118,94 @@ def tile_picked_ylopfw_shr_p_kernel(tc, x_words, x_scales, w1_words, w1_scales, 
         uh = sb("uh", [P, PACK], F32)
         nc.scalar.mul(uh[:], u[:], 0.5)
 
-        def by_member(ap):
-            return ap.rearrange("p (v d) -> p d v", d=D)
-
-        def rows(ap):
-            return ap.rearrange("p (d v) -> p d v", d=D)
+        def groups(ap):
+            return ap.rearrange("p (v d) -> p v d", d=D)
 
         def tiles(name):
             return [sb(f"{name}{t}", [P, S], F32) for t in range(PACK)]
 
-        prod, post, ex, cap, mag, gap, exc, sh = [tiles(n) for n in
-            ("prod", "post", "ex", "cap", "mag", "gap", "exc", "sh")]
+        prod, post, ex, cap, mag, gap, sh = [tiles(n) for n in
+            ("prod", "post", "ex", "cap", "mag", "gap", "sh")]
         def add_flow(t):
-            nc.vector.tensor_tensor(post[t][:].rearrange("p (d v) -> p v d", d=D),
-                                    prod[t][:].rearrange("p (v d) -> p v d", d=D),
-                                    fl_ps[t][:].rearrange("p (v d) -> p v d", d=D), ALU.add)
+            nc.vector.tensor_tensor(post[t][:], prod[t][:], fl_ps[t][:], ALU.add)
 
-        last = PACK - 1
-        for i, t in order[:-1]:
-            if i == 0:
-                nc.scalar.copy(fl[t][:, :S], fl_ps[t][:])
+        FUSED = 3
+        LATE = {}
+        def flow_copy(t):
+            nc.scalar.copy(fl[t][:, :S], fl_ps[t][:])
+
+        def other_case(t):
+            if t < FUSED:
+                nc.vector.tensor_tensor(prod[t][:], fl[t][:].indirect(outl_sb[:]), lo[t // 2][:, t % 2, :], ALU.mult)
             else:
-                nc.scalar.activation(rows(ex[t][:]), by_member(lm_ps[t][:]), ACT.Exp)
-        for t in range(last):
-            nc.vector.tensor_tensor(prod[t][:], fl[t][:].indirect(outl_sb[:]), lo[t // 2][:, t % 2, :], ALU.mult)
+                fo = sb(f"fo{t}", [P, S], F32)
+                nc.scalar.activation(fo[:], fl[t][:].indirect(outl_sb[:]), ACT.Copy)
+                nc.vector.tensor_tensor(prod[t][:], fo[:], lo[t // 2][:, t % 2, :], ALU.mult)
             add_flow(t)
+
+        for i, t in order:
+            if i == 0:
+                flow_copy(t)
+            else:
+                nc.scalar.activation(ex[t][:], lm_ps[t][:], ACT.Exp)
+        for t in range(PACK):
+            if t not in LATE.values():
+                other_case(t)
 
         th = sb("th", [P, PACK, S], F32)
         rcp = sb("rcp", [P, PACK, V], F32)
+        exc = sb("exc", [P, PACK, S], F32)
+        log_tot = th[:].rearrange("p t (a j) -> p t a j", a=PACK)[:, :, :, 0 : V // PACK]
         for t in range(PACK):
             ln = sb(f"ln{t}", [P, S], F32, tag=f"ex{t - 1}" if t else "ln0")
             nc.scalar.activation(ln[:], ex[t][:], ACT.Ln, bias=1.0)
             nc.scalar.activation(mag[t][:], post[t][:], ACT.Abs)
-            nc.vector.scalar_tensor_tensor(rows(cap[t][:]), rows(ln[:]), CLAMP, by_member(lm_ps[t][:]), ALU.min, ALU.max)
+            nc.vector.scalar_tensor_tensor(cap[t][:], ln[:], CLAMP, lm_ps[t][:], ALU.min, ALU.max)
             nc.vector.scalar_tensor_tensor(gap[t][:], mag[t][:], 0.5, cap[t][:], ALU.subtract, ALU.subtract)
-            upper = sb(f"upper{t}", [P, HALF], F32)
-            pairs = sb(f"pairs{t}", [P, HALF], F32)
+            over = exc[:, :, V * t : V * (t + 1)]
+            quarters = gap[t][:].rearrange("p (a j) -> p a j", a=PACK)
+            if t in (0, 1, 2, 3):
+                nc.scalar.activation(over, quarters, ACT.Relu)
+            else:
+                nc.vector.tensor_scalar(over, quarters, 0.0, None, ALU.max)
             tot = sb(f"tot{t}", [P, V], F32)
-            nc.vector.tensor_scalar(upper[:], gap[t][:, HALF:], 0.0, None, ALU.max)
-            nc.vector.scalar_tensor_tensor(pairs[:], gap[t][:, :HALF], 0.0, upper[:], ALU.max, ALU.add)
-            nc.vector.scalar_tensor_tensor(tot[:], pairs[:, :V], 0.3, pairs[:, V:], ALU.add, ALU.add)
-            nc.scalar.activation(th[:, t, 0:V], tot[:], ACT.Ln)
-            if t == 0:
-                nc.scalar.copy(fl[last][:, :S], fl_ps[last][:])
-                fo = sb("fo", [P, S], F32, tag="ln0")
-                nc.scalar.activation(fo[:], fl[last][:].indirect(outl_sb[:]), ACT.Copy)
-                nc.vector.tensor_tensor(prod[last][:], fo[:], lo[last // 2][:, last % 2, :], ALU.mult)
-                add_flow(last)
+            nc.vector.tensor_reduce(tot[:].rearrange("p (a v) -> p a v", a=PACK), over.rearrange("p a (v d) -> p a v d", d=D), mybir.AxisListType.X, ALU.add)
+            nc.scalar.activation(log_tot[:, t], tot[:].rearrange("p (a v) -> p a v", a=PACK), ACT.Ln, bias=0.3)
+            if t in LATE:
+                other_case(LATE[t])
         for t in range(PACK):
-            nc.vector.scalar_tensor_tensor(exc[t][:], gap[t][:], 0.0, post[t][:], ALU.max, ALU.mult)
-        nc.scalar.activation(rcp[:], th[:, :, 0:V], ACT.Exp, scale=-1.0)
-        for t in range(PACK):
-            nc.scalar.activation(th[:, t, :], post[t][:], ACT.Tanh)
-        for t in range(PACK):
-            nc.vector.scalar_tensor_tensor(rows(sh[t][:]), rows(exc[t][:]), u[:, t : t + 1],
-                                           rcp[:, t : t + 1, :].to_broadcast([P, D, V]), ALU.mult, ALU.mult)
-
-        out_ps = [psum.tile([P, S], F32, name=f"outb{m}", tag=f"bank0{m}") for m in range(N // P)]
-        for c in range(2):
-            cols = slice(c * HALF, (c + 1) * HALF)
-            hb = sb(f"hb{c}", [P, PACK, HALF], BF16)
+            nc.vector.scalar_tensor_tensor(exc[:, t, :], gap[t][:], 0.0, post[t][:], ALU.max, ALU.mult)
+        nc.scalar.activation(rcp[:].rearrange("p t (a v) -> p t a v", a=PACK), log_tot, ACT.Exp, scale=-1.0)
+        CHUNKS = [(0, 256), (256, 384), (384, 512)]
+        for lo_c, hi_c in CHUNKS:
+            for t in range(PACK):
+                nc.scalar.activation(th[:, t, lo_c:hi_c], post[t][:, lo_c:hi_c], ACT.Tanh)
+        for c, (lo_c, hi_c) in enumerate(CHUNKS):
+            cols = slice(lo_c, hi_c)
+            width = hi_c - lo_c
+            final = c == len(CHUNKS) - 1
+            hb = sb(f"hb{c}", [P, PACK, width], BF16)
+            for t in range(PACK):
+                nc.vector.scalar_tensor_tensor(groups(sh[t][:, cols]), groups(exc[:, t, cols]), u[:, t : t + 1],
+                                               rcp[:, t, lo_c // D : hi_c // D].unsqueeze(2).to_broadcast([P, width // D, D]), ALU.mult, ALU.mult)
             for t in range(PACK):
                 nc.vector.scalar_tensor_tensor(hb[:, t, :], th[:, t, cols], uh[:, t : t + 1], sh[t][:, cols], ALU.mult, ALU.add)
-            hi = sb(f"hi{c}", [P, HALF, PACK], BF16)
-            if c == 0:
+            hi = sb(f"hi{c}", [P, width, PACK], BF16)
+            if not final:
                 nc.scalar.copy(hi[:], hb[:].rearrange("p t j -> p j t"))
             else:
                 nc.vector.tensor_copy(hi[:], hb[:].rearrange("p t j -> p j t"))
-            hq = sb(f"hq{c}", [P, HALF], U32)
-            hs = sb(f"hs{c}", [P, HALF], U8)
+            hq = sb(f"hq{c}", [P, width], U32)
+            hs = sb(f"hs{c}", [P, width], U8)
             nc.vector.quantize_mx(out=hq[:].bitcast(FP8X4), scales=hs[:], in_=hi[:].rearrange("p j t -> p (j t)"))
             for m in range(N // P):
-                nc.tensor.matmul_mx(out=out_ps[m][:, cols], lhsT=w3w[:, 2 * P * m : 2 * P * (m + 1)].bitcast(FP4X4),
+                acc = psum.tile([P, width], F32, name=f"acc{c}{m}", tag=f"bank{c // 2}{2 * (c % 2) + m}")
+                nc.tensor.matmul_mx(out=acc[:], lhsT=w3w[:, 2 * P * m : 2 * P * (m + 1)].bitcast(FP4X4),
                                     lhsT_scale=w3s[:, 0, P * m : P * (m + 1)],
                                     rhs=hq[:].bitcast(FP8X4), rhs_scale=hs[:], start=True, stop=True)
-        for m in range(N // P):
-            res = sb(f"res{m}", [P, S], F32)
-            src = out_ps[m][:].rearrange("p (d v) -> p v d", d=D)
-            dst = res[:].rearrange("p (v d) -> p v d", d=D)
-            if m == 0:
-                nc.scalar.copy(dst, src)
-            else:
-                nc.vector.tensor_copy(dst, src)
-            (nc.scalar if m == 0 else nc.sync).dma_start(out=out[m * P : (m + 1) * P, :], in_=res[:])
+                res = sb(f"res{c}{m}", [P, width], F32)
+                if final and m == 1:
+                    nc.vector.tensor_copy(res[:], acc[:])
+                else:
+                    nc.scalar.copy(res[:], acc[:])
+                (nc.scalar if final and m == 0 else nc.sync).dma_start(out=out[m * P : (m + 1) * P, cols], in_=res[:])

@@ -42,7 +42,7 @@ def tile_picked_ylopfw_shr_p_kernel(tc, x_words, x_scales, w1_words, w1_scales, 
         offs_sb = sb("offs_sb", [P, S // 16], U16)
         outl_sb = sb("outl_sb", [P, S // 16], U16)
         xs = sb("xs", [P, T], U8)
-        raw_w = [sb(f"raw_w{i}", [P, PASSES, 2 * H], U8) for i in range(2)]
+        raw_w = [sb(f"raw_w{i}", [P, PASSES, 2 * H], U8, tag=f"stage{i}") for i in range(2)]
         raw_s = [sb(f"raw_s{i}", [P, PASSES, H], U8) for i in range(2)]
         gs = [sb(f"gs{g}", [P, S], U8) for g in range(PASSES)]
         dw = [sb(f"dw{i}", [P, PASSES, 2 * H], U8) for i in range(2)]
@@ -54,13 +54,13 @@ def tile_picked_ylopfw_shr_p_kernel(tc, x_words, x_scales, w1_words, w1_scales, 
             return tile
 
         def deal_words(i):
-            dst = dw[i][:].bitcast(U16).rearrange("p o (t m) -> p o t m", t=PACK)
-            src = raw_w[i][:].bitcast(U16).rearrange("p o (m t) -> p o t m", t=PACK)
+            dst = dw[i][:].bitcast(U16).rearrange("p o (t c i) -> p o c t i", t=PACK, i=8)
+            src = raw_w[i][:].bitcast(U16).rearrange("p o (c i t) -> p o c t i", t=PACK, i=8)
             nc.scalar.copy(dst, src)
 
         def deal_scales(i):
-            nc.vector.tensor_copy(out=ds[i][:].rearrange("p o (t m) -> p o t m", t=PACK),
-                                  in_=raw_s[i][:].rearrange("p o (m t) -> p o t m", t=PACK))
+            nc.vector.tensor_copy(out=ds[i][:].rearrange("p o (t c i) -> p o c t i", t=PACK, i=16),
+                                  in_=raw_s[i][:].rearrange("p o (c i t) -> p o c t i", t=PACK, i=16))
 
         fl = [sb(f"fl{t}", [P, S + 16], F32) for t in range(PACK)]
         nc.vector.memset(xs[:].bitcast(I32), 0)
@@ -72,16 +72,20 @@ def tile_picked_ylopfw_shr_p_kernel(tc, x_words, x_scales, w1_words, w1_scales, 
             nc.vector.memset(fl[t][:, S:], 0.0)
 
         nc.sync.dma_start(offs_sb[:], offs)
-        nc.sync.dma_start(outl_sb[:], out_l)
         nc.sync.dma_start(out=raw_w[0][:].bitcast(I32), in_=w1_words.rearrange("o p c -> p o c").bitcast(I32))
+        nc.sync.dma_start(out=raw_w[1][:].bitcast(I32), in_=w2_words.rearrange("o p c -> p o c").bitcast(I32))
         for q in range(4):
             nc.sync.dma_start(out=xs[32 * q : 32 * q + 8, :].bitcast(I32), in_=x_scales[:, 4 * q : 4 * q + 4, :].bitcast(I32))
         xw0 = load_x(0, "xw0")
         load_scale_rows(nc.sync, raw_s[0], w1_scales)
         xw1 = load_x(1, "xw1")
-        nc.sync.dma_start(out=raw_w[1][:].bitcast(I32), in_=w2_words.rearrange("o p c -> p o c").bitcast(I32))
+        nc.sync.dma_start(outl_sb[:], out_l)
 
         deal_words(0)
+        u = sb("u", [P, PACK], F32, tag="stage0")
+        nc.sync.dma_start(out=u[:], in_=unit.rearrange("(p t) o -> p (t o)", t=PACK))
+        uh = sb("uh", [P, PACK], F32)
+        nc.scalar.mul(uh[:], u[:], 0.5)
         nc.vector.tensor_copy(gs[0][:], xs[:].indirect(offs_sb[:]))
         for q in range(4):
             nc.sync.dma_start(out=gs[1][32 * q : 32 * q + 4, :].bitcast(I32), in_=gs[0][32 * q + 4 : 32 * q + 8, :].bitcast(I32))
@@ -113,10 +117,6 @@ def tile_picked_ylopfw_shr_p_kernel(tc, x_words, x_scales, w1_words, w1_scales, 
                                         rhs=gw[g][:].bitcast(FP8X4), rhs_scale=gs[g][:],
                                         start=(g == 0), stop=(g == PASSES - 1))
         fl_ps, lm_ps = banks
-        u = sb("u", [P, PACK], F32, tag="gs0")
-        nc.sync.dma_start(out=u[:], in_=unit.rearrange("(p t) o -> p (t o)", t=PACK))
-        uh = sb("uh", [P, PACK], F32)
-        nc.scalar.mul(uh[:], u[:], 0.5)
 
         def groups(ap):
             return ap.rearrange("p (v d) -> p v d", d=D)
@@ -175,9 +175,10 @@ def tile_picked_ylopfw_shr_p_kernel(tc, x_words, x_scales, w1_words, w1_scales, 
                 other_case(LATE[t])
         for t in range(PACK):
             nc.vector.scalar_tensor_tensor(exc[:, t, :], gap[t][:], 0.0, post[t][:], ALU.max, ALU.mult)
-        nc.scalar.activation(rcp[:].rearrange("p t (a v) -> p t a v", a=PACK), log_tot, ACT.Exp, scale=-1.0)
         CHUNKS = [(0, 256), (256, 384), (384, 512)]
         for lo_c, hi_c in CHUNKS:
+            blocks = slice(lo_c // V, hi_c // V)
+            nc.scalar.activation(rcp[:].rearrange("p t (a v) -> p t a v", a=PACK)[:, :, blocks, :], log_tot[:, :, blocks, :], ACT.Exp, scale=-1.0)
             for t in range(PACK):
                 nc.scalar.activation(th[:, t, lo_c:hi_c], post[t][:, lo_c:hi_c], ACT.Tanh)
         for c, (lo_c, hi_c) in enumerate(CHUNKS):
@@ -191,10 +192,12 @@ def tile_picked_ylopfw_shr_p_kernel(tc, x_words, x_scales, w1_words, w1_scales, 
             for t in range(PACK):
                 nc.vector.scalar_tensor_tensor(hb[:, t, :], th[:, t, cols], uh[:, t : t + 1], sh[t][:, cols], ALU.mult, ALU.add)
             hi = sb(f"hi{c}", [P, width, PACK], BF16)
+            dst = hi[:].rearrange("p (c i) t -> p c t i", i=4)
+            src = hb[:].rearrange("p t (c i) -> p c t i", i=4)
             if not final:
-                nc.scalar.copy(hi[:], hb[:].rearrange("p t j -> p j t"))
+                nc.scalar.copy(dst, src)
             else:
-                nc.vector.tensor_copy(hi[:], hb[:].rearrange("p t j -> p j t"))
+                nc.vector.tensor_copy(dst, src)
             hq = sb(f"hq{c}", [P, width], U32)
             hs = sb(f"hs{c}", [P, width], U8)
             nc.vector.quantize_mx(out=hq[:].bitcast(FP8X4), scales=hs[:], in_=hi[:].rearrange("p j t -> p (j t)"))

@@ -19,196 +19,197 @@ ACT = mybir.ActivationFunctionType
 P = 128
 PACK = 4
 PASSES = K // (P * PACK)
+QUADRANTS = 4
 V = S // D
-HALF = S // 2
-CLAMP = 40.0
+LAST = PACK - 1
+SPARE = 16
+LINE = 16
+SOFTPLUS_LINEAR = 40.0
+FLOW, LIMIT = 0, 1
+PRODUCTS = [(FLOW, t) for t in range(PACK)] + [(LIMIT, (t + 1) % PACK) for t in range(PACK)]
+CHUNKS = [(0, 256), (256, 384), (384, 512)]
 
 
 def tile_picked_ylopfw_shr_p_kernel(tc, x_words, x_scales, w1_words, w1_scales, w2_words, w2_scales,
-        lodf, unit, w3_words, w3_scales, offs, out_l, out):
+                                                                    lodf, unit, w3_words, w3_scales, offs, out_l, out):
     nc = tc.nc
     with ExitStack() as ctx:
         keep = ctx.enter_context(tc.tile_pool(name="keep", bufs=1))
         psum = ctx.enter_context(tc.psum_pool(name="psum", bufs=1))
 
-        def sb(name, shape, dtype, tag=None):
-            return keep.tile(shape, dtype, name=name, tag=tag or name, align_bytes=64)
+        def sb(name, shape, dtype, reuse=None):
+            return keep.tile(shape, dtype, name=name, tag=reuse or name, align_bytes=64)
+
+        def row_tiles(name):
+            return [sb(f"{name}{t}", [P, S], F32) for t in range(PACK)]
 
         def load_scale_rows(queue, tile, scales):
-            for q in range(4):
+            for q in range(QUADRANTS):
                 queue.dma_start(out=tile[32 * q : 32 * q + 4].bitcast(I32),
                                 in_=scales[:, 4 * q : 4 * q + 4, :].rearrange("o r c -> r o c").bitcast(I32))
 
-        offs_sb = sb("offs_sb", [P, S // 16], U16)
-        outl_sb = sb("outl_sb", [P, S // 16], U16)
-        xs = sb("xs", [P, T], U8)
-        raw_w = [sb(f"raw_w{i}", [P, PASSES, 2 * H], U8, tag=f"stage{i}") for i in range(2)]
-        raw_s = [sb(f"raw_s{i}", [P, PASSES, H], U8) for i in range(2)]
-        gs = [sb(f"gs{g}", [P, S], U8) for g in range(PASSES)]
-        dw = [sb(f"dw{i}", [P, PASSES, 2 * H], U8) for i in range(2)]
-        ds = [sb("ds0", [P, PASSES, H], U8)]
-
-        def load_x(g, tag):
-            tile = sb(f"xw{g}", [P, T], I32, tag=tag)
+        def load_x_words(g):
+            tile = sb(f"x_window{g}", [P, T], I32)
             nc.sync.dma_start(out=tile[:], in_=x_words[g].rearrange("p n t -> p (n t)").bitcast(I32))
             return tile
 
-        def deal_words(i):
-            dst = dw[i][:].bitcast(U16).rearrange("p o (t c i) -> p o c t i", t=PACK, i=8)
-            src = raw_w[i][:].bitcast(U16).rearrange("p o (c i t) -> p o c t i", t=PACK, i=8)
-            nc.scalar.copy(dst, src)
-
-        def deal_scales(i):
-            nc.vector.tensor_copy(out=ds[i][:].rearrange("p o (t c i) -> p o c t i", t=PACK, i=16),
-                                  in_=raw_s[i][:].rearrange("p o (c i t) -> p o c t i", t=PACK, i=16))
-
-        fl = [sb(f"fl{t}", [P, S + 16], F32) for t in range(PACK)]
-        nc.vector.memset(xs[:].bitcast(I32), 0)
-        nc.vector.memset(raw_s[0][:].bitcast(I32), 0)
-        nc.vector.memset(gs[1][:].bitcast(I32), 0)
-        nc.gpsimd.memset(raw_s[1][:].bitcast(I32), 0)
-        load_scale_rows(nc.gpsimd, raw_s[1], w2_scales)
-        for t in range(PACK):
-            nc.vector.memset(fl[t][:, S:], 0.0)
-
-        nc.sync.dma_start(offs_sb[:], offs)
-        nc.sync.dma_start(out=raw_w[0][:].bitcast(I32), in_=w1_words.rearrange("o p c -> p o c").bitcast(I32))
-        nc.sync.dma_start(out=raw_w[1][:].bitcast(I32), in_=w2_words.rearrange("o p c -> p o c").bitcast(I32))
-        for q in range(4):
-            nc.sync.dma_start(out=xs[32 * q : 32 * q + 8, :].bitcast(I32), in_=x_scales[:, 4 * q : 4 * q + 4, :].bitcast(I32))
-        xw0 = load_x(0, "xw0")
-        load_scale_rows(nc.sync, raw_s[0], w1_scales)
-        xw1 = load_x(1, "xw1")
-        nc.sync.dma_start(outl_sb[:], out_l)
-
-        deal_words(0)
-        u = sb("u", [P, PACK], F32, tag="stage0")
-        nc.sync.dma_start(out=u[:], in_=unit.rearrange("(p t) o -> p (t o)", t=PACK))
-        uh = sb("uh", [P, PACK], F32)
-        nc.scalar.mul(uh[:], u[:], 0.5)
-        nc.vector.tensor_copy(gs[0][:], xs[:].indirect(offs_sb[:]))
-        for q in range(4):
-            nc.sync.dma_start(out=gs[1][32 * q : 32 * q + 4, :].bitcast(I32), in_=gs[0][32 * q + 4 : 32 * q + 8, :].bitcast(I32))
-        lodf_v = lodf.rearrange("(p t) j -> p t j", t=PACK)
-        lo = [sb("lo0", [P, 2, S], F32, tag="xs")]
-        nc.sync.dma_start(out=lo[0][:], in_=lodf_v[:, 0:2, :])
-        gw = [sb(f"gw{g}", [P, S], U32) for g in range(PASSES)]
-        nc.vector.tensor_copy(gw[0][:], xw0[:].bitcast(U32).indirect(offs_sb[:]))
-        lo.append(sb("lo1", [P, 2, S], F32, tag="xw0"))
-        nc.sync.dma_start(out=lo[1][:], in_=lodf_v[:, 2:4, :])
-        deal_scales(0)
-        nc.vector.tensor_copy(gw[1][:], xw1[:].bitcast(U32).indirect(offs_sb[:]))
-        deal_words(1)
-        ds.append(sb("ds1", [P, PASSES, H], U8, tag="xw1"))
-        deal_scales(1)
-        w3w = raw_w[1][:, 0, 0 : 2 * N]
-        nc.sync.dma_start(out=w3w.bitcast(I32), in_=w3_words[0].bitcast(I32))
-        w3s = raw_s[1][:, 0:1, 0:N]
-        load_scale_rows(nc.sync, w3s, w3_scales)
-
-        banks = [[psum.tile([P, S], F32, name=f"bank{i}{t}", tag=f"bank{i}{t}") for t in range(PACK)] for i in range(2)]
-        order = [(0, 0), (0, 1), (1, 1), (1, 2), (0, 2), (1, 3), (1, 0), (0, 3)]
-        for i, t in order:
-            if True:
-                for g in range(PASSES):
-                    nc.tensor.matmul_mx(out=banks[i][t][:],
-                                        lhsT=dw[i][:, g, 2 * P * t : 2 * P * (t + 1)].bitcast(FP4X4),
-                                        lhsT_scale=ds[i][:, g, P * t : P * (t + 1)],
-                                        rhs=gw[g][:].bitcast(FP8X4), rhs_scale=gs[g][:],
-                                        start=(g == 0), stop=(g == PASSES - 1))
-        fl_ps, lm_ps = banks
+        def deal(dst, src, per_line, first=0, end=PACK):
+            nc.vector.tensor_copy(dst.rearrange("p o (t c i) -> p o c t i", t=end - first, i=per_line),
+                                  src.rearrange("p o (c i t) -> p o c t i", t=PACK, i=per_line)[:, :, :, first:end, :])
 
         def groups(ap):
             return ap.rearrange("p (v d) -> p v d", d=D)
 
-        def tiles(name):
-            return [sb(f"{name}{t}", [P, S], F32) for t in range(PACK)]
+        offs_sb = sb("offs_sb", [P, S // 16], U16)
+        out_l_sb = sb("out_l_sb", [P, S // 16], U16)
+        scale_window = sb("scale_window", [P, T], U8)
+        raw_words = [sb(f"raw_words{i}", [P, PASSES, 2 * H], U8) for i in (FLOW, LIMIT)]
+        raw_scales = [sb(f"raw_scales{i}", [P, PASSES, H], U8) for i in (FLOW, LIMIT)]
+        picked_scales = [sb(f"picked_scales{g}", [P, S], U8) for g in range(PASSES)]
+        w_words = [sb(f"w_words{i}", [P, PASSES, 2 * H], U8) for i in (FLOW, LIMIT)]
+        lead_scales = sb("lead_scales", [P, PASSES, P], U8)
+        rest_scales = sb("rest_scales", [P, PASSES, LAST * P], U8)
+        fl = [sb(f"fl{t}", [P, S + SPARE], F32) for t in range(PACK)]
 
-        prod, post, ex, cap, mag, gap, sh = [tiles(n) for n in
-            ("prod", "post", "ex", "cap", "mag", "gap", "sh")]
-        def add_flow(t):
-            nc.vector.tensor_tensor(post[t][:], prod[t][:], fl_ps[t][:], ALU.add)
-
-        FUSED = 3
-        LATE = {}
-        def flow_copy(t):
-            nc.scalar.copy(fl[t][:, :S], fl_ps[t][:])
-
-        def other_case(t):
-            if t < FUSED:
-                nc.vector.tensor_tensor(prod[t][:], fl[t][:].indirect(outl_sb[:]), lo[t // 2][:, t % 2, :], ALU.mult)
-            else:
-                fo = sb(f"fo{t}", [P, S], F32)
-                nc.scalar.activation(fo[:], fl[t][:].indirect(outl_sb[:]), ACT.Copy)
-                nc.vector.tensor_tensor(prod[t][:], fo[:], lo[t // 2][:, t % 2, :], ALU.mult)
-            add_flow(t)
-
-        for i, t in order:
-            if i == 0:
-                flow_copy(t)
-            else:
-                nc.scalar.activation(ex[t][:], lm_ps[t][:], ACT.Exp)
+        nc.vector.memset(scale_window[:].bitcast(I32), 0)
+        nc.vector.memset(raw_scales[FLOW][:].bitcast(I32), 0)
+        nc.vector.memset(picked_scales[1][:].bitcast(I32), 0)
+        nc.gpsimd.memset(raw_scales[LIMIT][:].bitcast(I32), 0)
+        load_scale_rows(nc.gpsimd, raw_scales[LIMIT], w2_scales)
         for t in range(PACK):
-            if t not in LATE.values():
-                other_case(t)
+            nc.vector.memset(fl[t][:, S:], 0.0)
 
-        th = sb("th", [P, PACK, S], F32)
-        rcp = sb("rcp", [P, PACK, V], F32)
-        exc = sb("exc", [P, PACK, S], F32)
-        log_tot = th[:].rearrange("p t (a j) -> p t a j", a=PACK)[:, :, :, 0 : V // PACK]
-        for t in range(PACK):
-            ln = sb(f"ln{t}", [P, S], F32, tag=f"ex{t - 1}" if t else "ln0")
-            nc.scalar.activation(ln[:], ex[t][:], ACT.Ln, bias=1.0)
-            nc.scalar.activation(mag[t][:], post[t][:], ACT.Abs)
-            nc.vector.scalar_tensor_tensor(cap[t][:], ln[:], CLAMP, lm_ps[t][:], ALU.min, ALU.max)
-            nc.vector.scalar_tensor_tensor(gap[t][:], mag[t][:], 0.5, cap[t][:], ALU.subtract, ALU.subtract)
-            over = exc[:, :, V * t : V * (t + 1)]
-            quarters = gap[t][:].rearrange("p (a j) -> p a j", a=PACK)
-            if t in (0, 1, 2, 3):
-                nc.scalar.activation(over, quarters, ACT.Relu)
+        nc.sync.dma_start(offs_sb[:], offs)
+        for i, words in ((FLOW, w1_words), (LIMIT, w2_words)):
+            nc.sync.dma_start(out=raw_words[i][:].bitcast(I32), in_=words.rearrange("o p c -> p o c").bitcast(I32))
+        for q in range(QUADRANTS):
+            nc.sync.dma_start(out=scale_window[32 * q : 32 * q + 8, :].bitcast(I32),
+                              in_=x_scales[:, 4 * q : 4 * q + 4, :].bitcast(I32))
+        x_window = [load_x_words(0)]
+        load_scale_rows(nc.sync, raw_scales[FLOW], w1_scales)
+        x_window.append(load_x_words(1))
+        nc.sync.dma_start(out_l_sb[:], out_l)
+
+        deal(w_words[FLOW][:].bitcast(U16), raw_words[FLOW][:].bitcast(U16), LINE // 2)
+        nc.vector.tensor_copy(picked_scales[0][:], scale_window[:].indirect(offs_sb[:]))
+        for q in range(QUADRANTS):
+            nc.sync.dma_start(out=picked_scales[1][32 * q : 32 * q + 4, :].bitcast(I32),
+                              in_=picked_scales[0][32 * q + 4 : 32 * q + 8, :].bitcast(I32))
+        deal(w_words[LIMIT][:].bitcast(U16), raw_words[LIMIT][:].bitcast(U16), LINE // 2)
+
+        lodf_rows = lodf.rearrange("(p t) j -> p t j", t=PACK)
+        factors = [sb("factors0", [P, 2, S], F32, reuse="scale_window")]
+        nc.sync.dma_start(out=factors[0][:], in_=lodf_rows[:, 0:2, :])
+        picked_words = [sb(f"picked_words{g}", [P, S], U32) for g in range(PASSES)]
+        nc.vector.tensor_copy(picked_words[0][:], x_window[0][:].bitcast(U32).indirect(offs_sb[:]))
+        factors.append(sb("factors1", [P, 2, S], F32, reuse="x_window0"))
+        nc.sync.dma_start(out=factors[1][:], in_=lodf_rows[:, 2:4, :])
+        deal(lead_scales[:], raw_scales[FLOW][:], LINE, 0, 1)
+        deal(rest_scales[:], raw_scales[FLOW][:], LINE, 1, PACK)
+        nc.vector.tensor_copy(picked_words[1][:], x_window[1][:].bitcast(U32).indirect(offs_sb[:]))
+
+        banks = [[psum.tile([P, S], F32, name=f"bank{i}{t}", tag=f"bank{i}{t}") for t in range(PACK)] for i in (FLOW, LIMIT)]
+
+        def product(i, t, scales):
+            for g in range(PASSES):
+                nc.tensor.matmul_mx(out=banks[i][t][:],
+                                    lhsT=w_words[i][:, g, 2 * P * t : 2 * P * (t + 1)].bitcast(FP4X4),
+                                    lhsT_scale=scales[:, g, :],
+                                    rhs=picked_words[g][:].bitcast(FP8X4), rhs_scale=picked_scales[g][:],
+                                    start=(g == 0), stop=(g == PASSES - 1))
+
+        product(*PRODUCTS[0], lead_scales)
+        limit_scales = sb("limit_scales", [P, PASSES, H], U8, reuse="lead_scales")
+        deal(limit_scales[:], raw_scales[LIMIT][:], LINE)
+        w3_scale_rows = raw_scales[LIMIT][:, 0:1, 0:N]
+        load_scale_rows(nc.sync, w3_scale_rows, w3_scales)
+        for i, t in PRODUCTS[1:]:
+            if i == FLOW:
+                product(i, t, rest_scales[:, :, P * (t - 1) : P * t])
             else:
-                nc.vector.tensor_scalar(over, quarters, 0.0, None, ALU.max)
-            tot = sb(f"tot{t}", [P, V], F32)
-            nc.vector.tensor_reduce(tot[:].rearrange("p (a v) -> p a v", a=PACK), over.rearrange("p a (v d) -> p a v d", d=D), mybir.AxisListType.X, ALU.add)
-            nc.scalar.activation(log_tot[:, t], tot[:].rearrange("p (a v) -> p a v", a=PACK), ACT.Ln, bias=0.3)
-            if t in LATE:
-                other_case(LATE[t])
-        for t in range(PACK):
-            nc.vector.scalar_tensor_tensor(exc[:, t, :], gap[t][:], 0.0, post[t][:], ALU.max, ALU.mult)
-        CHUNKS = [(0, 256), (256, 384), (384, 512)]
-        for lo_c, hi_c in CHUNKS:
-            blocks = slice(lo_c // V, hi_c // V)
-            nc.scalar.activation(rcp[:].rearrange("p t (a v) -> p t a v", a=PACK)[:, :, blocks, :], log_tot[:, :, blocks, :], ACT.Exp, scale=-1.0)
-            for t in range(PACK):
-                nc.scalar.activation(th[:, t, lo_c:hi_c], post[t][:, lo_c:hi_c], ACT.Tanh)
-        for c, (lo_c, hi_c) in enumerate(CHUNKS):
-            cols = slice(lo_c, hi_c)
-            width = hi_c - lo_c
-            final = c == len(CHUNKS) - 1
-            hb = sb(f"hb{c}", [P, PACK, width], BF16)
-            for t in range(PACK):
-                nc.vector.scalar_tensor_tensor(groups(sh[t][:, cols]), groups(exc[:, t, cols]), u[:, t : t + 1],
-                                               rcp[:, t, lo_c // D : hi_c // D].unsqueeze(2).to_broadcast([P, width // D, D]), ALU.mult, ALU.mult)
-            for t in range(PACK):
-                nc.vector.scalar_tensor_tensor(hb[:, t, :], th[:, t, cols], uh[:, t : t + 1], sh[t][:, cols], ALU.mult, ALU.add)
-            hi = sb(f"hi{c}", [P, width, PACK], BF16)
-            dst = hi[:].rearrange("p (c i) t -> p c t i", i=4)
-            src = hb[:].rearrange("p t (c i) -> p c t i", i=4)
-            if not final:
-                nc.scalar.copy(dst, src)
+                product(i, t, limit_scales[:, :, P * t : P * (t + 1)])
+        fl_psum, lm_psum = banks
+
+        w3_word_tile = sb("w3_word_tile", [P, 2 * N], U8, reuse="w_words0")
+        nc.sync.dma_start(out=w3_word_tile[:].bitcast(I32), in_=w3_words[0].bitcast(I32))
+        unit_sb = sb("unit_sb", [P, PACK], F32, reuse="picked_scales0")
+        nc.sync.dma_start(out=unit_sb[:], in_=unit.rearrange("(p t) o -> p (t o)", t=PACK))
+        half_unit = sb("half_unit", [P, PACK], F32)
+        nc.gpsimd.tensor_scalar(half_unit[:], unit_sb[:], 0.5, 0.0, ALU.mult, ALU.add)
+
+        shifted, post, exp_lm, cap, size, gap, share = [
+            row_tiles(name) for name in ("shifted", "post", "exp_lm", "cap", "size", "gap", "share")]
+
+        for i, t in PRODUCTS:
+            if i == LIMIT:
+                nc.scalar.activation(exp_lm[t][:], lm_psum[t][:], ACT.Exp)
             else:
+                nc.scalar.copy(fl[t][:, :S], fl_psum[t][:])
+
+        for t in range(PACK):
+            nc.vector.tensor_tensor(shifted[t][:], fl[t][:].indirect(out_l_sb[:]), factors[t // 2][:, t % 2, :], ALU.mult)
+            nc.vector.tensor_tensor(post[t][:], shifted[t][:], fl_psum[t][:], ALU.add)
+
+        tanh_post = sb("tanh_post", [P, PACK, S], F32)
+        inverse = sb("inverse", [P, PACK, V], F32)
+        excess = sb("excess", [P, PACK, S], F32)
+        total = sb("total", [P, PACK, PACK, V // PACK], F32)
+        log_total = tanh_post[:].rearrange("p t (a j) -> p t a j", a=PACK)[:, :, :, 0 : V // PACK]
+        for t in range(PACK):
+            soft = sb(f"soft{t}", [P, S], F32, reuse=f"exp_lm{t - 1}" if t else None)
+            nc.scalar.activation(soft[:], exp_lm[t][:], ACT.Ln, bias=1.0)
+            nc.scalar.activation(size[t][:], post[t][:], ACT.Abs)
+            nc.vector.scalar_tensor_tensor(cap[t][:], soft[:], SOFTPLUS_LINEAR, lm_psum[t][:], ALU.min, ALU.max)
+            nc.vector.scalar_tensor_tensor(gap[t][:], size[t][:], 0.5, cap[t][:], ALU.subtract, ALU.subtract)
+            over = excess[:, :, V * t : V * (t + 1)]
+            nc.scalar.activation(over, gap[t][:].rearrange("p (a j) -> p a j", a=PACK), ACT.Relu)
+            nc.vector.tensor_reduce(total[:, t], over.rearrange("p a (v d) -> p a v d", d=D), mybir.AxisListType.X, ALU.add)
+            if t == LAST - 1:
+                nc.scalar.activation(log_total[:, :LAST], total[:, :LAST], ACT.Ln, bias=0.3)
+            elif t == LAST:
+                nc.scalar.activation(log_total[:, LAST:], total[:, LAST:], ACT.Ln, bias=0.3)
+        for t in range(PACK):
+            nc.vector.scalar_tensor_tensor(excess[:, t, :], gap[t][:], 0.0, post[t][:], ALU.max, ALU.mult)
+
+        for first, end in CHUNKS:
+            quarters = slice(first // V, end // V)
+            nc.scalar.activation(inverse[:].rearrange("p t (a v) -> p t a v", a=PACK)[:, :, quarters, :],
+                                 log_total[:, :, quarters, :], ACT.Exp, scale=-1.0)
+            for t in range(PACK):
+                nc.scalar.activation(tanh_post[:, t, first:end], post[t][:, first:end], ACT.Tanh)
+
+        for c, (first, end) in enumerate(CHUNKS):
+            cols = slice(first, end)
+            width = end - first
+            tail = c == len(CHUNKS) - 1
+            hid = sb(f"hid{c}", [P, PACK, width], BF16)
+            for t in range(PACK):
+                per_group = inverse[:, t, first // D : end // D].unsqueeze(2).to_broadcast([P, width // D, D])
+                nc.vector.scalar_tensor_tensor(groups(share[t][:, cols]), groups(excess[:, t, cols]),
+                                               unit_sb[:, t : t + 1], per_group, ALU.mult, ALU.mult)
+            for t in range(PACK):
+                nc.vector.scalar_tensor_tensor(hid[:, t, :], tanh_post[:, t, cols], half_unit[:, t : t + 1],
+                                               share[t][:, cols], ALU.mult, ALU.add)
+            woven = sb(f"woven{c}", [P, width, PACK], BF16)
+            dst = woven[:].rearrange("p (c i) t -> p c t i", i=4)
+            src = hid[:].rearrange("p t (c i) -> p c t i", i=4)
+            if tail:
                 nc.vector.tensor_copy(dst, src)
-            hq = sb(f"hq{c}", [P, width], U32)
-            hs = sb(f"hs{c}", [P, width], U8)
-            nc.vector.quantize_mx(out=hq[:].bitcast(FP8X4), scales=hs[:], in_=hi[:].rearrange("p j t -> p (j t)"))
+            else:
+                nc.scalar.copy(dst, src)
+            hid_words = sb(f"hid_words{c}", [P, width], U32)
+            hid_scales = sb(f"hid_scales{c}", [P, width], U8)
+            nc.vector.quantize_mx(out=hid_words[:].bitcast(FP8X4), scales=hid_scales[:],
+                                  in_=woven[:].rearrange("p j t -> p (j t)"))
             for m in range(N // P):
                 acc = psum.tile([P, width], F32, name=f"acc{c}{m}", tag=f"bank{c // 2}{2 * (c % 2) + m}")
-                nc.tensor.matmul_mx(out=acc[:], lhsT=w3w[:, 2 * P * m : 2 * P * (m + 1)].bitcast(FP4X4),
-                                    lhsT_scale=w3s[:, 0, P * m : P * (m + 1)],
-                                    rhs=hq[:].bitcast(FP8X4), rhs_scale=hs[:], start=True, stop=True)
-                res = sb(f"res{c}{m}", [P, width], F32)
-                if final and m == 1:
-                    nc.vector.tensor_copy(res[:], acc[:])
+                nc.tensor.matmul_mx(out=acc[:], lhsT=w3_word_tile[:, 2 * P * m : 2 * P * (m + 1)].bitcast(FP4X4),
+                                    lhsT_scale=w3_scale_rows[:, 0, P * m : P * (m + 1)],
+                                    rhs=hid_words[:].bitcast(FP8X4), rhs_scale=hid_scales[:], start=True, stop=True)
+                result = sb(f"result{c}{m}", [P, width], F32)
+                if tail and m == 1:
+                    nc.vector.tensor_copy(result[:], acc[:])
                 else:
-                    nc.scalar.copy(res[:], acc[:])
-                (nc.scalar if final and m == 0 else nc.sync).dma_start(out=out[m * P : (m + 1) * P, cols], in_=res[:])
+                    nc.scalar.copy(result[:], acc[:])
+                queue = nc.scalar if tail and m == 0 else nc.sync
+                queue.dma_start(out=out[m * P : (m + 1) * P, cols], in_=result[:])

from contextlib import ExitStack

import concourse.mybir as mybir

K, T, S, D, N, H = 1024, 2048, 512, 4, 256, 512
FLOPS = 2 * (2 * K * H * S + H * N * S)

F32 = mybir.dt.float32
BF16 = mybir.dt.bfloat16
I32 = mybir.dt.int32
U32 = mybir.dt.uint32
U16 = mybir.dt.uint16
U8 = mybir.dt.uint8
FP8X4 = mybir.dt.float8_e4m3fn_x4
FP4X4 = mybir.dt.float4_e2m1fn_x4
ALU = mybir.AluOpType
ACT = mybir.ActivationFunctionType

P = 128
PACK = 4
PASSES = K // (P * PACK)
QUADRANTS = 4
V = S // D
LAST = PACK - 1
SPARE = 16
LINE = 16
SOFTPLUS_LINEAR = 40.0
FLOW, LIMIT = 0, 1
PRODUCTS = [(FLOW, t) for t in range(PACK)] + [(LIMIT, (t + 1) % PACK) for t in range(PACK)]
CHUNKS = [(0, 256), (256, 384), (384, 512)]


def tile_picked_ylopfw_shr_p_kernel(tc, x_words, x_scales, w1_words, w1_scales, w2_words, w2_scales,
                                                                    lodf, unit, w3_words, w3_scales, offs, out_l, out):
    nc = tc.nc
    with ExitStack() as ctx:
        keep = ctx.enter_context(tc.tile_pool(name="keep", bufs=1))
        psum = ctx.enter_context(tc.psum_pool(name="psum", bufs=1))

        def sb(name, shape, dtype, reuse=None):
            return keep.tile(shape, dtype, name=name, tag=reuse or name, align_bytes=64)

        def row_tiles(name):
            return [sb(f"{name}{t}", [P, S], F32) for t in range(PACK)]

        def load_scale_rows(queue, tile, scales):
            for q in range(QUADRANTS):
                queue.dma_start(out=tile[32 * q : 32 * q + 4].bitcast(I32),
                                in_=scales[:, 4 * q : 4 * q + 4, :].rearrange("o r c -> r o c").bitcast(I32))

        def load_x_words(g):
            tile = sb(f"x_window{g}", [P, T], I32)
            nc.sync.dma_start(out=tile[:], in_=x_words[g].rearrange("p n t -> p (n t)").bitcast(I32))
            return tile

        def deal(dst, src, per_line, first=0, end=PACK):
            nc.vector.tensor_copy(dst.rearrange("p o (t c i) -> p o c t i", t=end - first, i=per_line),
                                  src.rearrange("p o (c i t) -> p o c t i", t=PACK, i=per_line)[:, :, :, first:end, :])

        def groups(ap):
            return ap.rearrange("p (v d) -> p v d", d=D)

        offs_sb = sb("offs_sb", [P, S // 16], U16)
        out_l_sb = sb("out_l_sb", [P, S // 16], U16)
        scale_window = sb("scale_window", [P, T], U8)
        raw_words = [sb(f"raw_words{i}", [P, PASSES, 2 * H], U8) for i in (FLOW, LIMIT)]
        raw_scales = [sb(f"raw_scales{i}", [P, PASSES, H], U8) for i in (FLOW, LIMIT)]
        picked_scales = [sb(f"picked_scales{g}", [P, S], U8) for g in range(PASSES)]
        w_words = [sb(f"w_words{i}", [P, PASSES, 2 * H], U8) for i in (FLOW, LIMIT)]
        lead_scales = sb("lead_scales", [P, PASSES, P], U8)
        rest_scales = sb("rest_scales", [P, PASSES, LAST * P], U8)
        fl = [sb(f"fl{t}", [P, S + SPARE], F32) for t in range(PACK)]

        nc.vector.memset(scale_window[:].bitcast(I32), 0)
        nc.vector.memset(raw_scales[FLOW][:].bitcast(I32), 0)
        nc.vector.memset(picked_scales[1][:].bitcast(I32), 0)
        nc.gpsimd.memset(raw_scales[LIMIT][:].bitcast(I32), 0)
        load_scale_rows(nc.gpsimd, raw_scales[LIMIT], w2_scales)
        for t in range(PACK):
            nc.vector.memset(fl[t][:, S:], 0.0)

        nc.sync.dma_start(offs_sb[:], offs)
        for i, words in ((FLOW, w1_words), (LIMIT, w2_words)):
            nc.sync.dma_start(out=raw_words[i][:].bitcast(I32), in_=words.rearrange("o p c -> p o c").bitcast(I32))
        for q in range(QUADRANTS):
            nc.sync.dma_start(out=scale_window[32 * q : 32 * q + 8, :].bitcast(I32),
                              in_=x_scales[:, 4 * q : 4 * q + 4, :].bitcast(I32))
        x_window = [load_x_words(0)]
        load_scale_rows(nc.sync, raw_scales[FLOW], w1_scales)
        x_window.append(load_x_words(1))
        nc.sync.dma_start(out_l_sb[:], out_l)

        deal(w_words[FLOW][:].bitcast(U16), raw_words[FLOW][:].bitcast(U16), LINE // 2)
        nc.vector.tensor_copy(picked_scales[0][:], scale_window[:].indirect(offs_sb[:]))
        for q in range(QUADRANTS):
            nc.sync.dma_start(out=picked_scales[1][32 * q : 32 * q + 4, :].bitcast(I32),
                              in_=picked_scales[0][32 * q + 4 : 32 * q + 8, :].bitcast(I32))
        deal(w_words[LIMIT][:].bitcast(U16), raw_words[LIMIT][:].bitcast(U16), LINE // 2)

        lodf_rows = lodf.rearrange("(p t) j -> p t j", t=PACK)
        factors = [sb("factors0", [P, 2, S], F32, reuse="scale_window")]
        nc.sync.dma_start(out=factors[0][:], in_=lodf_rows[:, 0:2, :])
        picked_words = [sb(f"picked_words{g}", [P, S], U32) for g in range(PASSES)]
        nc.vector.tensor_copy(picked_words[0][:], x_window[0][:].bitcast(U32).indirect(offs_sb[:]))
        factors.append(sb("factors1", [P, 2, S], F32, reuse="x_window0"))
        nc.sync.dma_start(out=factors[1][:], in_=lodf_rows[:, 2:4, :])
        deal(lead_scales[:], raw_scales[FLOW][:], LINE, 0, 1)
        deal(rest_scales[:], raw_scales[FLOW][:], LINE, 1, PACK)
        nc.vector.tensor_copy(picked_words[1][:], x_window[1][:].bitcast(U32).indirect(offs_sb[:]))

        banks = [[psum.tile([P, S], F32, name=f"bank{i}{t}", tag=f"bank{i}{t}") for t in range(PACK)] for i in (FLOW, LIMIT)]

        def product(i, t, scales):
            for g in range(PASSES):
                nc.tensor.matmul_mx(out=banks[i][t][:],
                                    lhsT=w_words[i][:, g, 2 * P * t : 2 * P * (t + 1)].bitcast(FP4X4),
                                    lhsT_scale=scales[:, g, :],
                                    rhs=picked_words[g][:].bitcast(FP8X4), rhs_scale=picked_scales[g][:],
                                    start=(g == 0), stop=(g == PASSES - 1))

        product(*PRODUCTS[0], lead_scales)
        limit_scales = sb("limit_scales", [P, PASSES, H], U8, reuse="lead_scales")
        deal(limit_scales[:], raw_scales[LIMIT][:], LINE)
        w3_scale_rows = raw_scales[LIMIT][:, 0:1, 0:N]
        load_scale_rows(nc.sync, w3_scale_rows, w3_scales)
        for i, t in PRODUCTS[1:]:
            if i == FLOW:
                product(i, t, rest_scales[:, :, P * (t - 1) : P * t])
            else:
                product(i, t, limit_scales[:, :, P * t : P * (t + 1)])
        fl_psum, lm_psum = banks

        w3_word_tile = sb("w3_word_tile", [P, 2 * N], U8, reuse="w_words0")
        nc.sync.dma_start(out=w3_word_tile[:].bitcast(I32), in_=w3_words[0].bitcast(I32))
        unit_sb = sb("unit_sb", [P, PACK], F32, reuse="picked_scales0")
        nc.sync.dma_start(out=unit_sb[:], in_=unit.rearrange("(p t) o -> p (t o)", t=PACK))
        half_unit = sb("half_unit", [P, PACK], F32)
        nc.gpsimd.tensor_scalar(half_unit[:], unit_sb[:], 0.5, 0.0, ALU.mult, ALU.add)

        shifted, post, exp_lm, cap, size, gap, share = [
            row_tiles(name) for name in ("shifted", "post", "exp_lm", "cap", "size", "gap", "share")]

        for i, t in PRODUCTS:
            if i == LIMIT:
                nc.scalar.activation(exp_lm[t][:], lm_psum[t][:], ACT.Exp)
            else:
                nc.scalar.copy(fl[t][:, :S], fl_psum[t][:])

        for t in range(PACK):
            nc.vector.tensor_tensor(shifted[t][:], fl[t][:].indirect(out_l_sb[:]), factors[t // 2][:, t % 2, :], ALU.mult)
            nc.vector.tensor_tensor(post[t][:], shifted[t][:], fl_psum[t][:], ALU.add)

        tanh_post = sb("tanh_post", [P, PACK, S], F32)
        inverse = sb("inverse", [P, PACK, V], F32)
        excess = sb("excess", [P, PACK, S], F32)
        total = sb("total", [P, PACK, PACK, V // PACK], F32)
        log_total = tanh_post[:].rearrange("p t (a j) -> p t a j", a=PACK)[:, :, :, 0 : V // PACK]
        for t in range(PACK):
            soft = sb(f"soft{t}", [P, S], F32, reuse=f"exp_lm{t - 1}" if t else None)
            nc.scalar.activation(soft[:], exp_lm[t][:], ACT.Ln, bias=1.0)
            nc.scalar.activation(size[t][:], post[t][:], ACT.Abs)
            nc.vector.scalar_tensor_tensor(cap[t][:], soft[:], SOFTPLUS_LINEAR, lm_psum[t][:], ALU.min, ALU.max)
            nc.vector.scalar_tensor_tensor(gap[t][:], size[t][:], 0.5, cap[t][:], ALU.subtract, ALU.subtract)
            over = excess[:, :, V * t : V * (t + 1)]
            nc.scalar.activation(over, gap[t][:].rearrange("p (a j) -> p a j", a=PACK), ACT.Relu)
            nc.vector.tensor_reduce(total[:, t], over.rearrange("p a (v d) -> p a v d", d=D), mybir.AxisListType.X, ALU.add)
            if t == LAST - 1:
                nc.scalar.activation(log_total[:, :LAST], total[:, :LAST], ACT.Ln, bias=0.3)
            elif t == LAST:
                nc.scalar.activation(log_total[:, LAST:], total[:, LAST:], ACT.Ln, bias=0.3)
        for t in range(PACK):
            nc.vector.scalar_tensor_tensor(excess[:, t, :], gap[t][:], 0.0, post[t][:], ALU.max, ALU.mult)

        for first, end in CHUNKS:
            quarters = slice(first // V, end // V)
            nc.scalar.activation(inverse[:].rearrange("p t (a v) -> p t a v", a=PACK)[:, :, quarters, :],
                                 log_total[:, :, quarters, :], ACT.Exp, scale=-1.0)
            for t in range(PACK):
                nc.scalar.activation(tanh_post[:, t, first:end], post[t][:, first:end], ACT.Tanh)

        for c, (first, end) in enumerate(CHUNKS):
            cols = slice(first, end)
            width = end - first
            tail = c == len(CHUNKS) - 1
            hid = sb(f"hid{c}", [P, PACK, width], BF16)
            for t in range(PACK):
                per_group = inverse[:, t, first // D : end // D].unsqueeze(2).to_broadcast([P, width // D, D])
                nc.vector.scalar_tensor_tensor(groups(share[t][:, cols]), groups(excess[:, t, cols]),
                                               unit_sb[:, t : t + 1], per_group, ALU.mult, ALU.mult)
            for t in range(PACK):
                nc.vector.scalar_tensor_tensor(hid[:, t, :], tanh_post[:, t, cols], half_unit[:, t : t + 1],
                                               share[t][:, cols], ALU.mult, ALU.add)
            woven = sb(f"woven{c}", [P, width, PACK], BF16)
            dst = woven[:].rearrange("p (c i) t -> p c t i", i=4)
            src = hid[:].rearrange("p t (c i) -> p c t i", i=4)
            if tail:
                nc.vector.tensor_copy(dst, src)
            else:
                nc.scalar.copy(dst, src)
            hid_words = sb(f"hid_words{c}", [P, width], U32)
            hid_scales = sb(f"hid_scales{c}", [P, width], U8)
            nc.vector.quantize_mx(out=hid_words[:].bitcast(FP8X4), scales=hid_scales[:],
                                  in_=woven[:].rearrange("p j t -> p (j t)"))
            for m in range(N // P):
                acc = psum.tile([P, width], F32, name=f"acc{c}{m}", tag=f"bank{c // 2}{2 * (c % 2) + m}")
                nc.tensor.matmul_mx(out=acc[:], lhsT=w3_word_tile[:, 2 * P * m : 2 * P * (m + 1)].bitcast(FP4X4),
                                    lhsT_scale=w3_scale_rows[:, 0, P * m : P * (m + 1)],
                                    rhs=hid_words[:].bitcast(FP8X4), rhs_scale=hid_scales[:], start=True, stop=True)
                result = sb(f"result{c}{m}", [P, width], F32)
                if tail and m == 1:
                    nc.vector.tensor_copy(result[:], acc[:])
                else:
                    nc.scalar.copy(result[:], acc[:])
                queue = nc.scalar if tail and m == 0 else nc.sync
                queue.dma_start(out=out[m * P : (m + 1) * P, cols], in_=result[:])
